import numpy as np
import ml_dtypes


def mxq(x, axis, fmt="e4m3"):
    dtype, down = {"e4m3": (ml_dtypes.float8_e4m3fn, 7), "e5m2": (ml_dtypes.float8_e5m2, 14)}[fmt]
    v = np.moveaxis(np.asarray(x, np.float32).astype(ml_dtypes.bfloat16).astype(np.float64), axis, -1)
    blocks = v.reshape(v.shape[:-1] + (-1, 32))
    amax = np.abs(blocks).max(-1, keepdims=True)
    byte = np.maximum(np.where(amax > 0, np.frexp(amax)[1] - 1 + 127, 0) - down, 1)
    scale = np.exp2(byte - 127.0)
    codes = (blocks / scale).astype(np.float32).astype(dtype).astype(np.float64)
    return np.moveaxis((codes * scale).reshape(v.shape), -1, axis)


WIDE = False


def mx_kscale(k):
    if not WIDE:
        return np.ones(k)
    levels = np.array([10, -10, 5, -5, 0])
    if k % 512:
        return np.exp2(np.random.permutation(np.resize(levels, k // 32))).repeat(32)
    a = np.empty((k // 512, 16))
    for p in range(k // 512):
        a[p, :8] = np.random.permutation(np.resize(levels, 8))
        for g in range(8):
            far = levels[np.abs(levels - a[p, g]) >= 10]
            a[p, g + 8] = far[np.random.randint(len(far))]
    return np.exp2(a.ravel()).repeat(32)


def f64(x):
    return np.asarray(x).astype(np.float64)


def striped(idx):
    return np.tile(idx.reshape(-1, 16).T, (8, 1)).astype(np.uint16)


def unstriped(offs):
    return offs[:16].T.reshape(-1).astype(np.int64)


def striped8(idx):
    return np.concatenate([x.reshape(-1, 16).T for x in idx]).astype(np.uint16)


def runs(offs, k):
    lists = np.stack([offs[16 * r : 16 * r + 16].T.reshape(-1) for r in range(8)]).astype(np.int64)
    return lists[np.arange(k) % 512 // 64]


def pack_weight(w):
    k, n = w.shape
    w = f64(np.asarray(w, np.float32).astype(ml_dtypes.bfloat16)).reshape(k // 32, 32, n)
    amax = np.abs(w).max(1)
    byte = np.clip(np.where(amax > 0, np.frexp(amax)[1] - 1 + 127 - 7, 1), 1, 254)
    scaled = (w * np.exp2(127.0 - byte)[:, None, :]).reshape(k, n).astype(np.float32)
    words = np.ascontiguousarray(scaled.reshape(k // 512, 128, 4, n).transpose(0, 1, 3, 2)).astype(ml_dtypes.float8_e4m3fn).view(np.uint8)
    return words, np.ascontiguousarray(byte.astype(np.uint8).reshape(k // 512, 16, n))


def unpack_weight(words, scales):
    g, p, n, _ = words.shape
    vals = np.ascontiguousarray(words).view(ml_dtypes.float8_e4m3fn).astype(np.float64) * np.repeat(np.exp2(scales.astype(np.float64) - 127.0), 8, axis=1)[..., None]
    return vals.transpose(0, 1, 3, 2).reshape(g * 512, n)


E2M1 = np.array([0.0, 0.5, 1.0, 1.5, 2.0, 3.0, 4.0, 6.0, -0.0, -0.5, -1.0, -1.5, -2.0, -3.0, -4.0, -6.0])


def pack_fp4(w):
    k, n = w.shape
    w = f64(np.asarray(w, np.float32).astype(ml_dtypes.bfloat16)).reshape(k // 32, 32, n)
    amax = np.abs(w).max(1)
    mant, ex = np.frexp(amax / 6.0)
    byte = np.clip(np.where(amax > 0, np.where(mant > 0.5, ex, ex - 1) + 127, 1), 1, 254)
    scaled = (w * np.exp2(127.0 - byte)[:, None, :]).reshape(k, n).astype(np.float32)
    c = np.ascontiguousarray(scaled.reshape(k // 512, 128, 4, n).transpose(0, 1, 3, 2)).astype(ml_dtypes.float4_e2m1fn).view(np.uint8) & 0xF
    words = (c[..., 0::2] | (c[..., 1::2] << 4)).reshape(k // 512, 128, 2 * n)
    return np.ascontiguousarray(words), np.ascontiguousarray(byte.astype(np.uint8).reshape(k // 512, 16, n))


def unpack_fp4(words, scales):
    g, _, n = scales.shape
    words = np.ascontiguousarray(words).reshape(g, 128, n, 2)
    nib = np.empty((g, 128, n, 4), np.uint8)
    nib[..., 0::2] = words & 0xF
    nib[..., 1::2] = words >> 4
    vals = E2M1[nib] * np.repeat(np.exp2(scales.astype(np.float64) - 127.0), 8, axis=1)[..., None]
    return vals.transpose(0, 1, 3, 2).reshape(g * 512, n)


def sigmoid(v):
    return 1.0 / (1.0 + np.exp(-np.maximum(v, -700.0)))

def planes(y):
    n, m = y.shape
    v = y.astype(np.float32).astype(ml_dtypes.bfloat16).astype(np.float64).reshape(n // 32, 32, m)
    top = np.abs(v).max(1)
    byte = np.clip(np.where(top > 0, np.frexp(top)[1] - 1 + 127 - 7, 1), 1, 254)
    codes = (v * np.exp2(127.0 - byte)[:, None, :]).reshape(n, m).astype(np.float32).astype(ml_dtypes.float8_e4m3fn).view(np.uint8)
    words = codes.reshape(n // 512, 128, 4, m).transpose(0, 1, 3, 2)
    return np.ascontiguousarray(words), np.ascontiguousarray(byte.astype(np.uint8).reshape(n // 512, 16, m))


K, T, S, V, G, H = 512, 1024, 512, 512, 2048, 512


def setup_inputs():
    n = np.random.standard_normal
    s = mx_kscale(K)[:, None]
    u = mx_kscale(S)
    packed_xT = pack_weight(n((K, T)) * s)
    packed_dT = pack_weight(n((K, G)) / s)
    packed_w1 = pack_fp4(n((K, H)) / np.sqrt(K) / s)
    return {
        "x_words": packed_xT[0],
        "x_scales": packed_xT[1],
        "d_words": packed_dT[0],
        "d_scales": packed_dT[1],
        "w1_words": packed_w1[0],
        "w1_scales": packed_w1[1],
        "ga": (np.random.uniform(0.5, 1.5, (H, 1)) * u[:, None]).astype(np.float32),
        "gb": (np.random.uniform(0.5, 1.5, (H, 1)) / u[:, None]).astype(np.float32),
        "offs": striped(np.random.permutation(T)[:S]),
        "k1": striped8(np.random.randint(0, G, (8, H))),
        "two": striped(np.random.permutation(T)[:V]),
        "n1": striped8(np.stack([np.random.permutation(S) for _ in range(8)])),
        "n2": striped8(np.stack([np.random.permutation(V) for _ in range(8)])),
        "n3": striped8(np.stack([np.random.permutation(V) for _ in range(8)])),
        "n4": striped8(np.stack([np.random.permutation(V) for _ in range(8)])),
        "n5": striped8(np.stack([np.random.permutation(V) for _ in range(8)])),
        "n6": striped8(np.stack([np.random.permutation(V) for _ in range(8)])),
    }


def reference(x_words, x_scales, d_words, d_scales, w1_words, w1_scales, ga, gb, offs, k1, two, n1, n2, n3, n4, n5, n6):
    d_k1 = unpack_weight(d_words, d_scales)[np.arange(K)[:, None], runs(k1, K)]
    xq = unpack_weight(x_words, x_scales)[:, unstriped(offs)]
    a = 0.0625 * (d_k1.T @ xq)
    z = f64(ga) * (a * (sigmoid(a[np.arange(H)[:, None], runs(n1, H)])))
    x_two = unpack_weight(x_words, x_scales)[:, unstriped(two)]
    b = unpack_fp4(w1_words, w1_scales).T @ x_two
    z2 = f64(gb) * (b * (b[np.arange(H)[:, None], runs(n2, H)] - (b[np.arange(H)[:, None], runs(n3, H)])))
    s = 0.0625 * ((mxq(z, 0, "e4m3").T @ mxq(z2, 0, "e4m3")))
    out_0 = np.maximum(s, s[np.arange(S)[:, None], runs(n4, S)]) - (np.maximum(s[np.arange(S)[:, None], runs(n5, S)], s[np.arange(S)[:, None], runs(n6, S)]))
    return (out_0,) + planes(out_0)

@@ -1,0 +1,224 @@
+from contextlib import ExitStack
+
+import concourse.mybir as mybir
+from concourse.masks import make_identity
+
+F32 = mybir.dt.float32
+BF16 = mybir.dt.bfloat16
+I32 = mybir.dt.int32
+U32 = mybir.dt.uint32
+U16 = mybir.dt.uint16
+U8 = mybir.dt.uint8
+FP8X4 = mybir.dt.float8_e4m3fn_x4
+FP4X4 = mybir.dt.float4_e2m1fn_x4
+ALU = mybir.AluOpType
+ACT = mybir.ActivationFunctionType
+
+P = 128
+PACK = 4
+N = 512
+T = 1024
+G = 2048
+HALF = 256
+OUT_CHUNKS = (256, 128, 128)
+FLOPS = 3 * 2 * 512 * 512 * 512
+
+
+def tile_picked_ckqgatewindmix_none_po_kernel(tc, x_words, x_scales, d_words, d_scales, w1_words, w1_scales, ga, gb,
+        offs, k1, two, n1, n2, n3, n4, n5, n6, out_0, out_1, out_2):
+    nc = tc.nc
+    with ExitStack() as ctx:
+        lists = ctx.enter_context(tc.tile_pool(name="lists", bufs=1))
+        keep = ctx.enter_context(tc.tile_pool(name="keep", bufs=1))
+        psum = ctx.enter_context(tc.psum_pool(name="psum", bufs=1))
+
+        def sb(shape, dtype, name):
+            return keep.tile(shape, dtype, name=name, align_bytes=64)
+
+        def bank(i, name):
+            return psum.tile([P, N], F32, name=name, tag="bank%d" % i)
+
+        def load_list(src, name):
+            tile = lists.tile([P, N // 16], U16, name=name)
+            nc.sync.dma_start(tile[:], src)
+            return tile
+
+        def load_plane(src, width, name):
+            tile = sb([P, width], U8, name)
+            rows = src[0].bitcast(I32)
+            for q in range(4):
+                view = rows[4 * q:4 * q + 4, :].unsqueeze(0).broadcast_to([8, 4, width // 4])
+                nc.sync.dma_start(tile[:].bitcast(I32)[32 * q:32 * (q + 1), :], view)
+            return tile
+
+        def load_words(src, words, name):
+            tile = sb([P, words], I32, name)
+            nc.sync.dma_start(tile[:], src.bitcast(I32))
+            return tile
+
+        def gather(out, window, offsets):
+            nc.vector.tensor_copy(out, window.indirect(offsets))
+
+        def deal(src, run, name):
+            width = src.shape[1]
+            tile = sb([P, width], I32, name)
+            nc.vector.tensor_copy(
+                tile[:].rearrange("p (t b w) -> p t b w", t=PACK, w=run),
+                src.rearrange("p (b t w) -> p t b w", t=PACK, w=run))
+            return tile
+
+        l_two = load_list(two, "l_two")
+        xs = load_plane(x_scales, T, "xs")
+        xw = load_words(x_words[0].rearrange("p c r -> p (c r)"), T, "xw")
+        l_offs = load_list(offs, "l_offs")
+        l_k1 = load_list(k1, "l_k1")
+        ds = sb([P, G], U8, "ds")
+        nc.sync.dma_start(ds[:].bitcast(I32), d_scales[0].bitcast(I32).unsqueeze(1).broadcast_to([16, 8, G // 4]))
+        w1w = load_words(w1_words[0], N // 2, "w1w")
+        w1s = load_plane(w1_scales, N, "w1s")
+        dw = load_words(d_words[0].rearrange("p c r -> p (c r)"), G, "dw")
+        l_n3 = load_list(n3, "l_n3")
+        l_n2 = load_list(n2, "l_n2")
+        l_n1 = load_list(n1, "l_n1")
+        l_n4 = load_list(n4, "l_n4")
+        l_n5 = load_list(n5, "l_n5")
+        l_n6 = load_list(n6, "l_n6")
+
+        ident = sb([P, P], F32, "ident")
+        make_identity(nc, ident[:])
+        grows = sb([P, P], F32, "grows")
+        nc.gpsimd.memset(grows[:], 0.0)
+        for i, g in enumerate((ga, gb)):
+            nc.gpsimd.dma_start(
+                grows[PACK * i:PACK * (i + 1), :].rearrange("t (b e) -> t b e", e=8),
+                g.rearrange("(b t e) o -> t b (e o)", t=PACK, e=8))
+        warm = sb([P, 1], F32, "warm")
+        nc.scalar.activation(warm[:], ident[:, 0:1], ACT.Sigmoid)
+        gps = bank(7, "gps")
+        nc.tensor.transpose(gps[:, 0:P], grows[:], ident[:])
+        gcol = sb([P, 2 * PACK], F32, "gcol")
+
+        x2s = sb([P, N], U8, "x2s")
+        gather(x2s[:], xs[:], l_two[:])
+        x2w = sb([P, N], I32, "x2w")
+        gather(x2w[:].bitcast(U32), xw[:].bitcast(U32), l_two[:])
+        w1wd = deal(w1w[:], 4, "w1wd")
+        w1sd = deal(w1s[:].bitcast(I32), 2, "w1sd")
+        b_ps = [bank(t, "b_ps%d" % t) for t in range(PACK)]
+        b_win = [sb([P, N], F32, "b_win%d" % t) for t in range(PACK)]
+        for t in range(PACK):
+            nc.tensor.matmul_mx(
+                b_ps[t][:],
+                lhsT=w1wd[:].bitcast(U8)[:, 2 * P * t:2 * P * (t + 1)].bitcast(FP4X4),
+                lhsT_scale=w1sd[:].bitcast(U8)[:, P * t:P * (t + 1)],
+                rhs=x2w[:].bitcast(FP8X4), rhs_scale=x2s[:], start=True, stop=True)
+            nc.scalar.activation(b_win[t][:], b_ps[t][:], ACT.Copy)
+        nc.scalar.activation(gcol[:], gps[:, 0:2 * PACK], ACT.Copy)
+        b_gain = sb([P, PACK, N], F32, "b_gain")
+        for t in range(PACK):
+            nc.scalar.activation(b_gain[:, t, :], b_ps[t][:], ACT.Copy, scale=gcol[:, PACK + t:PACK + t + 1])
+
+        dsg = sb([P, N], U8, "dsg")
+        gather(dsg[:], ds[:], l_k1[:])
+        ds_odd = deal(dsg[:].bitcast(I32), 2, "ds_odd")
+        dsd = deal(dsg[:].bitcast(I32), 2, "dsd")
+        for r in range(1, 4):
+            nc.sync.dma_start(dsd[r:P:32, :], ds_odd[8 * r:P:32, :])
+        x1s = sb([P, N], U8, "x1s")
+        gather(x1s[:], xs[:], l_offs[:])
+        x1w = sb([P, N], I32, "x1w")
+        gather(x1w[:].bitcast(U32), xw[:].bitcast(U32), l_offs[:])
+        dwg = sb([P, N], I32, "dwg")
+        gather(dwg[:].bitcast(U32), dw[:].bitcast(U32), l_k1[:])
+        dwd = deal(dwg[:], 8, "dwd")
+        a_win = [sb([P, N], F32, "a_win%d" % t) for t in range(PACK)]
+        a_gain = sb([P, PACK, N], F32, "a_gain")
+        gate = sb([P, PACK, N], F32, "gate")
+        for t in range(PACK):
+            a_ps = bank(4 + t, "a_ps%d" % t)
+            nc.tensor.matmul_mx(
+                a_ps[:],
+                lhsT=dwd[:, P * t:P * (t + 1)].bitcast(FP8X4),
+                lhsT_scale=dsd[:].bitcast(U8)[:, P * t:P * (t + 1)],
+                rhs=x1w[:].bitcast(FP8X4), rhs_scale=x1s[:], start=True, stop=True)
+            nc.scalar.activation(a_win[t][:], a_ps[:], ACT.Copy, scale=0.0625)
+            for h in range(2):
+                nc.scalar.activation(gate[:, t, HALF * h:HALF * (h + 1)],
+                                     a_win[t][:].indirect(l_n1[:, 16 * h:16 * (h + 1)]), ACT.Sigmoid)
+            nc.scalar.activation(a_gain[:, t, :], a_win[t][:], ACT.Copy, scale=gcol[:, t:t + 1])
+
+        z2w = sb([P, N], I32, "z2w")
+        z2s = sb([P, N], U8, "z2s")
+        nc.gpsimd.memset(z2s[:], 0)
+        for h in range(2):
+            cols = slice(HALF * h, HALF * (h + 1))
+            lcols = slice(16 * h, 16 * (h + 1))
+            b3 = sb([P, PACK, HALF], F32, "b3_%d" % h)
+            diff = sb([P, PACK, HALF], F32, "diff%d" % h)
+            for t in range(PACK):
+                gather(b3[:, t, :], b_win[t][:], l_n3[:, lcols])
+            for t in range(PACK):
+                nc.vector.tensor_tensor(diff[:, t, :], b_win[t][:].indirect(l_n2[:, lcols]), b3[:, t, :], ALU.subtract)
+            z2b = sb([P, HALF * PACK], BF16, "z2b%d" % h)
+            nc.vector.tensor_tensor(
+                z2b[:].rearrange("p (c i t) -> p c t i", i=2, t=PACK),
+                diff[:].rearrange("p t (c i) -> p c t i", i=2),
+                b_gain[:, :, cols].rearrange("p t (c i) -> p c t i", i=2), ALU.mult)
+            nc.vector.quantize_mx(z2w[:, cols].bitcast(FP8X4), z2s[:, cols], z2b[:])
+
+        s_win = [sb([P, N], F32, "s_win%d" % t) for t in range(PACK)]
+        for h in range(2):
+            zb = sb([P, HALF * PACK], BF16, "zb%d" % h)
+            nc.vector.tensor_tensor(
+                zb[:].rearrange("p (u m t) -> p m t u", u=2, t=PACK),
+                gate[:].rearrange("p t (m u) -> p m t u", u=PACK)[:, :, :, 2 * h:2 * h + 2],
+                a_gain[:].rearrange("p t (m u) -> p m t u", u=PACK)[:, :, :, 2 * h:2 * h + 2], ALU.mult)
+            zw = sb([P, HALF], I32, "zw%d" % h)
+            zs = sb([P, HALF], U8, "zs%d" % h)
+            nc.gpsimd.memset(zs[:], 0)
+            nc.vector.quantize_mx(zw[:].bitcast(FP8X4), zs[:], zb[:])
+            for u in range(2):
+                t = 2 * h + u
+                s_ps = bank(t, "s_ps%d" % t)
+                nc.tensor.matmul_mx(
+                    s_ps[:],
+                    lhsT=zw[:, P * u:P * (u + 1)].bitcast(FP8X4), lhsT_scale=zs[:, P * u:P * (u + 1)],
+                    rhs=z2w[:].bitcast(FP8X4), rhs_scale=z2s[:], start=True, stop=True)
+                nc.scalar.activation(s_win[t][:], s_ps[:], ACT.Copy, scale=-0.0625)
+
+        ow = sb([P, N], I32, "ow")
+        osc = sb([P, N], U8, "osc")
+        out_rows = out_0.rearrange("(p t) v -> p t v", t=PACK)
+        out_words = out_1[0].rearrange("p c r -> p (c r)").bitcast(I32)
+        start = 0
+        for c, width in enumerate(OUT_CHUNKS):
+            cols = slice(start, start + width)
+            lcols = slice(start // 16, (start + width) // 16)
+            start = start + width
+            s4 = sb([P, PACK, width], F32, "s4_%d" % c)
+            low = sb([P, PACK, width], F32, "low%d" % c)
+            f5 = sb([P, PACK, width], F32, "f5_%d" % c)
+            f6 = sb([P, PACK, width], F32, "f6_%d" % c)
+            res = sb([P, PACK, width], F32, "res%d" % c)
+            for t in range(PACK):
+                gather(s4[:, t, :], s_win[t][:], l_n4[:, lcols])
+            for t in range(PACK):
+                nc.vector.tensor_tensor(low[:, t, :], s_win[t][:, cols], s4[:, t, :], ALU.min)
+            for t in range(PACK):
+                nc.vector.tensor_tensor(f5[:, t, :], s_win[t][:].indirect(l_n5[:, lcols]), low[:, t, :], ALU.subtract)
+            for t in range(PACK):
+                nc.vector.tensor_tensor(f6[:, t, :], s_win[t][:].indirect(l_n6[:, lcols]), low[:, t, :], ALU.subtract)
+            nc.vector.tensor_tensor(res[:], f5[:], f6[:], ALU.min)
+            nc.sync.dma_start(out_rows[:, :, cols], res[:])
+            rb = sb([P, width * PACK], BF16, "rb%d" % c)
+            dst = rb[:].rearrange("p (c i t) -> p c t i", i=4, t=PACK)
+            src = res[:].rearrange("p t (c i) -> p c t i", i=4)
+            if c + 1 < len(OUT_CHUNKS):
+                nc.scalar.copy(dst, src)
+            else:
+                nc.vector.tensor_copy(dst, src)
+            nc.vector.quantize_mx(ow[:, cols].bitcast(FP8X4), osc[:, cols], rb[:])
+            nc.sync.dma_start(out_words[:, cols], ow[:, cols])
+        out_scales = out_2[0].bitcast(I32)
+        for r in range(4):
+            nc.sync.dma_start(out_scales[r:16:4, :], osc[:].bitcast(I32)[r:P:32, :])

@@ -20,7 +20,6 @@ N = 512
 T = 1024
 G = 2048
 HALF = 256
-OUT_CHUNKS = (256, 128, 128)
 FLOPS = 3 * 2 * 512 * 512 * 512
 
 
@@ -32,8 +31,8 @@ def tile_picked_ckqgatewindmix_none_po_kernel(tc, x_words, x_scales, d_words, d_
         keep = ctx.enter_context(tc.tile_pool(name="keep", bufs=1))
         psum = ctx.enter_context(tc.psum_pool(name="psum", bufs=1))
 
-        def sb(shape, dtype, name):
-            return keep.tile(shape, dtype, name=name, align_bytes=64)
+        def sb(shape, dtype, name, tag=""):
+            return keep.tile(shape, dtype, name=name, tag=tag or name, align_bytes=64)
 
         def bank(i, name):
             return psum.tile([P, N], F32, name=name, tag="bank%d" % i)
@@ -43,12 +42,17 @@ def tile_picked_ckqgatewindmix_none_po_kernel(tc, x_words, x_scales, d_words, d_
             nc.sync.dma_start(tile[:], src)
             return tile
 
-        def load_plane(src, width, name):
+        def load_plane(queue, src, width, name):
             tile = sb([P, width], U8, name)
             rows = src[0].bitcast(I32)
             for q in range(4):
                 view = rows[4 * q:4 * q + 4, :].unsqueeze(0).broadcast_to([8, 4, width // 4])
-                nc.sync.dma_start(tile[:].bitcast(I32)[32 * q:32 * (q + 1), :], view)
+                queue.dma_start(tile[:].bitcast(I32)[32 * q:32 * (q + 1), :], view)
+            return tile
+
+        def window(engine, name):
+            tile = sb([P, 2 * N], F32, name)
+            engine.memset(tile[:, N:], 0.0)
             return tile
 
         def load_words(src, words, name):
@@ -68,14 +72,14 @@ def tile_picked_ckqgatewindmix_none_po_kernel(tc, x_words, x_scales, d_words, d_
             return tile
 
         l_two = load_list(two, "l_two")
-        xs = load_plane(x_scales, T, "xs")
+        xs = load_plane(nc.scalar, x_scales, T, "xs")
         xw = load_words(x_words[0].rearrange("p c r -> p (c r)"), T, "xw")
-        l_offs = load_list(offs, "l_offs")
+        w1w = load_words(w1_words[0], N // 2, "w1w")
         l_k1 = load_list(k1, "l_k1")
+        w1s = load_plane(nc.sync, w1_scales, N, "w1s")
         ds = sb([P, G], U8, "ds")
         nc.sync.dma_start(ds[:].bitcast(I32), d_scales[0].bitcast(I32).unsqueeze(1).broadcast_to([16, 8, G // 4]))
-        w1w = load_words(w1_words[0], N // 2, "w1w")
-        w1s = load_plane(w1_scales, N, "w1s")
+        l_offs = load_list(offs, "l_offs")
         dw = load_words(d_words[0].rearrange("p c r -> p (c r)"), G, "dw")
         l_n3 = load_list(n3, "l_n3")
         l_n2 = load_list(n2, "l_n2")
@@ -84,19 +88,20 @@ def tile_picked_ckqgatewindmix_none_po_kernel(tc, x_words, x_scales, d_words, d_
         l_n5 = load_list(n5, "l_n5")
         l_n6 = load_list(n6, "l_n6")
 
-        ident = sb([P, P], F32, "ident")
-        make_identity(nc, ident[:])
         grows = sb([P, P], F32, "grows")
         nc.gpsimd.memset(grows[:], 0.0)
         for i, g in enumerate((ga, gb)):
             nc.gpsimd.dma_start(
                 grows[PACK * i:PACK * (i + 1), :].rearrange("t (b e) -> t b e", e=8),
                 g.rearrange("(b t e) o -> t b (e o)", t=PACK, e=8))
-        warm = sb([P, 1], F32, "warm")
-        nc.scalar.activation(warm[:], ident[:, 0:1], ACT.Sigmoid)
-        gps = bank(7, "gps")
-        nc.tensor.transpose(gps[:, 0:P], grows[:], ident[:])
+        ident = sb([P, P], F32, "ident")
+        make_identity(nc, ident[:])
         gcol = sb([P, 2 * PACK], F32, "gcol")
+
+        b_win = [window(nc.vector, "b_win%d" % t) for t in range(PACK)]
+        warm = sb([P, 1], F32, "warm")
+        nc.scalar.activation(warm[:], b_win[0][:, N:N + 1], ACT.Sigmoid)
+        s_win = [window(nc.gpsimd, "s_win%d" % t) for t in range(PACK)]
 
         x2s = sb([P, N], U8, "x2s")
         gather(x2s[:], xs[:], l_two[:])
@@ -104,31 +109,32 @@ def tile_picked_ckqgatewindmix_none_po_kernel(tc, x_words, x_scales, d_words, d_
         gather(x2w[:].bitcast(U32), xw[:].bitcast(U32), l_two[:])
         w1wd = deal(w1w[:], 4, "w1wd")
         w1sd = deal(w1s[:].bitcast(I32), 2, "w1sd")
-        b_ps = [bank(t, "b_ps%d" % t) for t in range(PACK)]
-        b_win = [sb([P, N], F32, "b_win%d" % t) for t in range(PACK)]
-        for t in range(PACK):
-            nc.tensor.matmul_mx(
-                b_ps[t][:],
-                lhsT=w1wd[:].bitcast(U8)[:, 2 * P * t:2 * P * (t + 1)].bitcast(FP4X4),
-                lhsT_scale=w1sd[:].bitcast(U8)[:, P * t:P * (t + 1)],
-                rhs=x2w[:].bitcast(FP8X4), rhs_scale=x2s[:], start=True, stop=True)
-            nc.scalar.activation(b_win[t][:], b_ps[t][:], ACT.Copy)
-        nc.scalar.activation(gcol[:], gps[:, 0:2 * PACK], ACT.Copy)
-        b_gain = sb([P, PACK, N], F32, "b_gain")
-        for t in range(PACK):
-            nc.scalar.activation(b_gain[:, t, :], b_ps[t][:], ACT.Copy, scale=gcol[:, PACK + t:PACK + t + 1])
-
         dsg = sb([P, N], U8, "dsg")
         gather(dsg[:], ds[:], l_k1[:])
         ds_odd = deal(dsg[:].bitcast(I32), 2, "ds_odd")
         dsd = deal(dsg[:].bitcast(I32), 2, "dsd")
         for r in range(1, 4):
             nc.sync.dma_start(dsd[r:P:32, :], ds_odd[8 * r:P:32, :])
+        b_ps = [bank(t, "b_ps%d" % t) for t in range(PACK)]
+        for t in range(PACK):
+            nc.tensor.matmul_mx(
+                b_ps[t][:],
+                lhsT=w1wd[:].bitcast(U8)[:, 2 * P * t:2 * P * (t + 1)].bitcast(FP4X4),
+                lhsT_scale=w1sd[:].bitcast(U8)[:, P * t:P * (t + 1)],
+                rhs=x2w[:].bitcast(FP8X4), rhs_scale=x2s[:], start=True, stop=True)
+            nc.scalar.activation(b_win[t][:, :N], b_ps[t][:], ACT.Copy)
+        gps = bank(7, "gps")
+        nc.tensor.transpose(gps[:, 0:P], grows[:], ident[:])
+        nc.scalar.activation(gcol[:], gps[:, 0:2 * PACK], ACT.Copy)
+        b_gain = sb([P, PACK, N], F32, "b_gain")
+        for t in range(PACK):
+            nc.scalar.activation(b_gain[:, t, :], b_ps[t][:], ACT.Copy, scale=gcol[:, PACK + t:PACK + t + 1])
+
         x1s = sb([P, N], U8, "x1s")
         gather(x1s[:], xs[:], l_offs[:])
         x1w = sb([P, N], I32, "x1w")
         gather(x1w[:].bitcast(U32), xw[:].bitcast(U32), l_offs[:])
-        dwg = sb([P, N], I32, "dwg")
+        dwg = sb([P, N], I32, "dwg", "dwg_b3")
         gather(dwg[:].bitcast(U32), dw[:].bitcast(U32), l_k1[:])
         dwd = deal(dwg[:], 8, "dwd")
         a_win = [sb([P, N], F32, "a_win%d" % t) for t in range(PACK)]
@@ -147,78 +153,98 @@ def tile_picked_ckqgatewindmix_none_po_kernel(tc, x_words, x_scales, d_words, d_
                                      a_win[t][:].indirect(l_n1[:, 16 * h:16 * (h + 1)]), ACT.Sigmoid)
             nc.scalar.activation(a_gain[:, t, :], a_win[t][:], ACT.Copy, scale=gcol[:, t:t + 1])
 
-        z2w = sb([P, N], I32, "z2w")
-        z2s = sb([P, N], U8, "z2s")
-        nc.gpsimd.memset(z2s[:], 0)
-        for h in range(2):
-            cols = slice(HALF * h, HALF * (h + 1))
-            lcols = slice(16 * h, 16 * (h + 1))
-            b3 = sb([P, PACK, HALF], F32, "b3_%d" % h)
-            diff = sb([P, PACK, HALF], F32, "diff%d" % h)
-            for t in range(PACK):
-                gather(b3[:, t, :], b_win[t][:], l_n3[:, lcols])
-            for t in range(PACK):
-                nc.vector.tensor_tensor(diff[:, t, :], b_win[t][:].indirect(l_n2[:, lcols]), b3[:, t, :], ALU.subtract)
-            z2b = sb([P, HALF * PACK], BF16, "z2b%d" % h)
-            nc.vector.tensor_tensor(
-                z2b[:].rearrange("p (c i t) -> p c t i", i=2, t=PACK),
-                diff[:].rearrange("p t (c i) -> p c t i", i=2),
-                b_gain[:, :, cols].rearrange("p t (c i) -> p c t i", i=2), ALU.mult)
-            nc.vector.quantize_mx(z2w[:, cols].bitcast(FP8X4), z2s[:, cols], z2b[:])
+        b3 = sb([P, PACK, N], F32, "b3", "dwg_b3")
+        diff = sb([P, PACK, N], F32, "diff")
+        for t in range(PACK):
+            gather(b3[:, t, :], b_win[t][:], l_n3[:])
+        for t in range(PACK):
+            nc.vector.tensor_tensor(diff[:, t, :], b_win[t][:].indirect(l_n2[:]), b3[:, t, :], ALU.subtract)
+        zb = [sb([P, HALF * PACK], BF16, "zb%d" % h) for h in range(2)]
+        zw = [sb([P, HALF], I32, "zw%d" % h) for h in range(2)]
+        zs = [sb([P, HALF], U8, "zs%d" % h) for h in range(2)]
 
-        s_win = [sb([P, N], F32, "s_win%d" % t) for t in range(PACK)]
-        for h in range(2):
-            zb = sb([P, HALF * PACK], BF16, "zb%d" % h)
+        def z_product(h):
             nc.vector.tensor_tensor(
-                zb[:].rearrange("p (u m t) -> p m t u", u=2, t=PACK),
+                zb[h][:].rearrange("p (u m t) -> p m t u", u=2, t=PACK),
                 gate[:].rearrange("p t (m u) -> p m t u", u=PACK)[:, :, :, 2 * h:2 * h + 2],
                 a_gain[:].rearrange("p t (m u) -> p m t u", u=PACK)[:, :, :, 2 * h:2 * h + 2], ALU.mult)
-            zw = sb([P, HALF], I32, "zw%d" % h)
-            zs = sb([P, HALF], U8, "zs%d" % h)
-            nc.gpsimd.memset(zs[:], 0)
-            nc.vector.quantize_mx(zw[:].bitcast(FP8X4), zs[:], zb[:])
-            for u in range(2):
-                t = 2 * h + u
-                s_ps = bank(t, "s_ps%d" % t)
-                nc.tensor.matmul_mx(
-                    s_ps[:],
-                    lhsT=zw[:, P * u:P * (u + 1)].bitcast(FP8X4), lhsT_scale=zs[:, P * u:P * (u + 1)],
-                    rhs=z2w[:].bitcast(FP8X4), rhs_scale=z2s[:], start=True, stop=True)
-                nc.scalar.activation(s_win[t][:], s_ps[:], ACT.Copy, scale=-0.0625)
+
+        def z_quantise(h):
+            nc.vector.quantize_mx(zw[h][:].bitcast(FP8X4), zs[h][:], zb[h][:])
+
+        z2b = sb([P, N * PACK], BF16, "z2b")
+        z2w = sb([P, N], I32, "z2w")
+        z2s = sb([P, N], U8, "z2s")
+        nc.vector.tensor_tensor(
+            z2b[:].rearrange("p (c i t) -> p c t i", i=2, t=PACK),
+            diff[:].rearrange("p t (c i) -> p c t i", i=2),
+            b_gain[:].rearrange("p t (c i) -> p c t i", i=2), ALU.mult)
+        z_product(0)
+        nc.vector.quantize_mx(z2w[:].bitcast(FP8X4), z2s[:], z2b[:])
+        z_quantise(0)
+        z_product(1)
+        z_quantise(1)
+        for t in range(PACK):
+            h, u = divmod(t, 2)
+            s_ps = bank(t, "s_ps%d" % t)
+            nc.tensor.matmul_mx(
+                s_ps[:],
+                lhsT=zw[h][:, P * u:P * (u + 1)].bitcast(FP8X4), lhsT_scale=zs[h][:, P * u:P * (u + 1)],
+                rhs=z2w[:].bitcast(FP8X4), rhs_scale=z2s[:], start=True, stop=True)
+            nc.scalar.activation(s_win[t][:, :N], s_ps[:], ACT.Copy, scale=-0.0625)
 
         ow = sb([P, N], I32, "ow")
         osc = sb([P, N], U8, "osc")
+        s4 = sb([P, PACK, N], F32, "s4")
+        low = sb([P, PACK, N], F32, "low")
+        f5 = sb([P, PACK, N], F32, "f5")
+        f6 = sb([P, PACK, N], F32, "f6")
+        res = sb([P, PACK, N], F32, "res")
         out_rows = out_0.rearrange("(p t) v -> p t v", t=PACK)
         out_words = out_1[0].rearrange("p c r -> p (c r)").bitcast(I32)
-        start = 0
-        for c, width in enumerate(OUT_CHUNKS):
-            cols = slice(start, start + width)
-            lcols = slice(start // 16, (start + width) // 16)
-            start = start + width
-            s4 = sb([P, PACK, width], F32, "s4_%d" % c)
-            low = sb([P, PACK, width], F32, "low%d" % c)
-            f5 = sb([P, PACK, width], F32, "f5_%d" % c)
-            f6 = sb([P, PACK, width], F32, "f6_%d" % c)
-            res = sb([P, PACK, width], F32, "res%d" % c)
-            for t in range(PACK):
-                gather(s4[:, t, :], s_win[t][:], l_n4[:, lcols])
-            for t in range(PACK):
-                nc.vector.tensor_tensor(low[:, t, :], s_win[t][:, cols], s4[:, t, :], ALU.min)
-            for t in range(PACK):
-                nc.vector.tensor_tensor(f5[:, t, :], s_win[t][:].indirect(l_n5[:, lcols]), low[:, t, :], ALU.subtract)
-            for t in range(PACK):
-                nc.vector.tensor_tensor(f6[:, t, :], s_win[t][:].indirect(l_n6[:, lcols]), low[:, t, :], ALU.subtract)
-            nc.vector.tensor_tensor(res[:], f5[:], f6[:], ALU.min)
-            nc.sync.dma_start(out_rows[:, :, cols], res[:])
-            rb = sb([P, width * PACK], BF16, "rb%d" % c)
-            dst = rb[:].rearrange("p (c i t) -> p c t i", i=4, t=PACK)
-            src = res[:].rearrange("p t (c i) -> p c t i", i=4)
-            if c + 1 < len(OUT_CHUNKS):
-                nc.scalar.copy(dst, src)
-            else:
-                nc.vector.tensor_copy(dst, src)
+
+        def first_steps(t, lo, hi):
+            gather(s4[:, t, lo:hi], s_win[t][:], l_n4[:, lo // 16:hi // 16])
+
+        def second_steps(t, lo, hi):
+            nc.vector.tensor_tensor(low[:, t, lo:hi], s_win[t][:, lo:hi], s4[:, t, lo:hi], ALU.min)
+
+        def third_steps(t, lo, hi):
+            for f, lst in ((f5, l_n5), (f6, l_n6)):
+                nc.vector.tensor_tensor(f[:, t, lo:hi], s_win[t][:].indirect(lst[:, lo // 16:hi // 16]),
+                                        low[:, t, lo:hi], ALU.subtract)
+
+        def last_steps(t, lo, hi):
+            nc.vector.tensor_tensor(res[:, t, lo:hi], f5[:, t, lo:hi], f6[:, t, lo:hi], ALU.min)
+            nc.sync.dma_start(out_rows[:, t, lo:hi], res[:, t, lo:hi])
+
+        def round_half(copy, h):
+            rb = sb([P, HALF * PACK], BF16, "rb%d" % h)
+            copy(rb[:].rearrange("p (c i t) -> p c t i", i=4, t=PACK),
+                 res[:, :, HALF * h:HALF * (h + 1)].rearrange("p t (c i) -> p c t i", i=4))
+            return rb
+
+        def planes(rb, h):
+            cols = slice(HALF * h, HALF * (h + 1))
             nc.vector.quantize_mx(ow[:, cols].bitcast(FP8X4), osc[:, cols], rb[:])
             nc.sync.dma_start(out_words[:, cols], ow[:, cols])
+
+        pieces = [(0, 0, N), (1, 0, N), (2, 0, N), (3, 0, HALF), (3, HALF, N)]
+        first_steps(*pieces[0])
+        first_steps(*pieces[1])
+        second_steps(*pieces[0])
+        for i, piece in enumerate(pieces):
+            if i + 2 < len(pieces):
+                first_steps(*pieces[i + 2])
+            third_steps(*piece)
+            if i + 1 < len(pieces):
+                second_steps(*pieces[i + 1])
+            last_steps(*piece)
+            if i + 2 == len(pieces):
+                rb0 = round_half(nc.scalar.copy, 0)
+        rb1 = round_half(nc.vector.tensor_copy, 1)
+        planes(rb0, 0)
+        planes(rb1, 1)
         out_scales = out_2[0].bitcast(I32)
         for r in range(4):
-            nc.sync.dma_start(out_scales[r:16:4, :], osc[:].bitcast(I32)[r:P:32, :])
+            (nc.scalar, nc.sync)[r % 2].dma_start(out_scales[r:16:4, :], osc[:].bitcast(I32)[r:P:32, :])

@@ -101,7 +101,10 @@ def tile_picked_ckqgatewindmix_none_po_kernel(tc, x_words, x_scales, d_words, d_
         b_win = [window(nc.vector, "b_win%d" % t) for t in range(PACK)]
         warm = sb([P, 1], F32, "warm")
         nc.scalar.activation(warm[:], b_win[0][:, N:N + 1], ACT.Sigmoid)
-        s_win = [window(nc.gpsimd, "s_win%d" % t) for t in range(PACK)]
+        neg_win = [window(nc.gpsimd, "neg_win%d" % t) for t in range(PACK)]
+        pos_win = [sb([P, 2 * N], F32, "pos_win%d" % t) for t in range(PACK)]
+        for t in range(PACK):
+            nc.scalar.copy(pos_win[t][:, N:], b_win[0][:, N:])
 
         x2s = sb([P, N], U8, "x2s")
         gather(x2s[:], xs[:], l_two[:])
@@ -184,38 +187,53 @@ def tile_picked_ckqgatewindmix_none_po_kernel(tc, x_words, x_scales, d_words, d_
         z_quantise(0)
         z_product(1)
         z_quantise(1)
-        for t in range(PACK):
+
+        def s_rows(t):
             h, u = divmod(t, 2)
             s_ps = bank(t, "s_ps%d" % t)
             nc.tensor.matmul_mx(
                 s_ps[:],
                 lhsT=zw[h][:, P * u:P * (u + 1)].bitcast(FP8X4), lhsT_scale=zs[h][:, P * u:P * (u + 1)],
                 rhs=z2w[:].bitcast(FP8X4), rhs_scale=z2s[:], start=True, stop=True)
-            nc.scalar.activation(s_win[t][:, :N], s_ps[:], ACT.Copy, scale=-0.0625)
+            nc.scalar.activation(neg_win[t][:, :N], s_ps[:], ACT.Copy, scale=-0.0625)
+            nc.scalar.activation(pos_win[t][:, :N], s_ps[:], ACT.Copy, scale=0.0625)
 
         ow = sb([P, N], I32, "ow")
         osc = sb([P, N], U8, "osc")
-        s4 = sb([P, PACK, N], F32, "s4")
-        low = sb([P, PACK, N], F32, "low")
-        f5 = sb([P, PACK, N], F32, "f5")
-        f6 = sb([P, PACK, N], F32, "f6")
+        neg5 = sb([P, PACK, N], F32, "neg5")
+        turned = sb([P, PACK, N], F32, "turned")
         res = sb([P, PACK, N], F32, "res")
         out_rows = out_0.rearrange("(p t) v -> p t v", t=PACK)
         out_words = out_1[0].rearrange("p c r -> p (c r)").bitcast(I32)
 
-        def first_steps(t, lo, hi):
-            gather(s4[:, t, lo:hi], s_win[t][:], l_n4[:, lo // 16:hi // 16])
+        def lead(t):
+            gather(neg5[:, t, :], neg_win[t][:], l_n5[:])
+            rise = sb([P, N], F32, "rise%d" % t, "slot%d" % t)
+            nc.vector.tensor_tensor(rise[:], pos_win[t][:].indirect(l_n4[:]), neg_win[t][:, :N], ALU.add)
+            excess = keep.tile([P, N], F32, name="excess%d" % t, tag="excess", bufs=2)
+            nc.scalar.activation(excess[:], rise[:], ACT.Relu)
+            sum_ps = bank(4 + t, "sum_ps%d" % t)
+            terms = (pos_win[t][:, :N], neg5[:, t, :], excess[:])
+            for k in range(PACK):
+                for i, term in enumerate(terms):
+                    nc.tensor.matmul(sum_ps[:, P * k:P * (k + 1)], lhsT=term[:, P * k:P * (k + 1)], rhs=ident[:],
+                                     is_transpose=True, start=(i == 0), stop=(i == len(terms) - 1))
+            nc.scalar.copy(turned[:, t, :], sum_ps[:])
+            lead_ps = bank(t, "lead_ps%d" % t)
+            for k in range(PACK):
+                nc.tensor.transpose(lead_ps[:, P * k:P * (k + 1)], turned[:, t, P * k:P * (k + 1)], ident[:])
+            return lead_ps
 
-        def second_steps(t, lo, hi):
-            nc.vector.tensor_tensor(low[:, t, lo:hi], s_win[t][:, lo:hi], s4[:, t, lo:hi], ALU.min)
+        def gap_step(i):
+            t, lo, hi = pieces[i]
+            gap = sb([P, hi - lo], F32, "gap%d" % i, "slot%d" % (2 + t % 2))
+            nc.vector.tensor_tensor(gap[:], neg_win[t][:].indirect(l_n6[:, lo // 16:hi // 16]),
+                                    neg5[:, t, lo:hi], ALU.subtract)
+            return gap
 
-        def third_steps(t, lo, hi):
-            for f, lst in ((f5, l_n5), (f6, l_n6)):
-                nc.vector.tensor_tensor(f[:, t, lo:hi], s_win[t][:].indirect(lst[:, lo // 16:hi // 16]),
-                                        low[:, t, lo:hi], ALU.subtract)
-
-        def last_steps(t, lo, hi):
-            nc.vector.tensor_tensor(res[:, t, lo:hi], f5[:, t, lo:hi], f6[:, t, lo:hi], ALU.min)
+        def last_step(i, gap):
+            t, lo, hi = pieces[i]
+            nc.vector.scalar_tensor_tensor(res[:, t, lo:hi], gap[:], 0.0, leads[t][:, lo:hi], ALU.min, ALU.add)
             nc.sync.dma_start(out_rows[:, t, lo:hi], res[:, t, lo:hi])
 
         def round_half(copy, h):
@@ -230,18 +248,20 @@ def tile_picked_ckqgatewindmix_none_po_kernel(tc, x_words, x_scales, d_words, d_
             nc.sync.dma_start(out_words[:, cols], ow[:, cols])
 
         pieces = [(0, 0, N), (1, 0, N), (2, 0, N), (3, 0, HALF), (3, HALF, N)]
-        first_steps(*pieces[0])
-        first_steps(*pieces[1])
-        second_steps(*pieces[0])
-        for i, piece in enumerate(pieces):
-            if i + 2 < len(pieces):
-                first_steps(*pieces[i + 2])
-            third_steps(*piece)
-            if i + 1 < len(pieces):
-                second_steps(*pieces[i + 1])
-            last_steps(*piece)
-            if i + 2 == len(pieces):
-                rb0 = round_half(nc.scalar.copy, 0)
+        leads = []
+        s_rows(0)
+        for t in range(PACK):
+            if t + 1 < PACK:
+                s_rows(t + 1)
+            leads.append(lead(t))
+        gap = gap_step(0)
+        for i in range(PACK - 1):
+            next_gap = gap_step(i + 1)
+            last_step(i, gap)
+            gap = next_gap
+        last_step(PACK - 1, gap)
+        rb0 = round_half(nc.scalar.copy, 0)
+        last_step(PACK, gap_step(PACK))
         rb1 = round_half(nc.vector.tensor_copy, 1)
         planes(rb0, 0)
         planes(rb1, 1)

@@ -20,6 +20,7 @@ N = 512
 T = 1024
 G = 2048
 HALF = 256
+GAP_SLOTS = ("slot2", "slot3", "turned0", "turned1", "turned3")
 FLOPS = 3 * 2 * 512 * 512 * 512
 
 
@@ -72,7 +73,7 @@ def tile_picked_ckqgatewindmix_none_po_kernel(tc, x_words, x_scales, d_words, d_
             return tile
 
         l_two = load_list(two, "l_two")
-        xs = load_plane(nc.scalar, x_scales, T, "xs")
+        xs = load_plane(nc.sync, x_scales, T, "xs")
         xw = load_words(x_words[0].rearrange("p c r -> p (c r)"), T, "xw")
         w1w = load_words(w1_words[0], N // 2, "w1w")
         l_k1 = load_list(k1, "l_k1")
@@ -99,12 +100,10 @@ def tile_picked_ckqgatewindmix_none_po_kernel(tc, x_words, x_scales, d_words, d_
         gcol = sb([P, 2 * PACK], F32, "gcol")
 
         b_win = [window(nc.vector, "b_win%d" % t) for t in range(PACK)]
-        warm = sb([P, 1], F32, "warm")
-        nc.scalar.activation(warm[:], b_win[0][:, N:N + 1], ACT.Sigmoid)
         neg_win = [window(nc.gpsimd, "neg_win%d" % t) for t in range(PACK)]
         pos_win = [sb([P, 2 * N], F32, "pos_win%d" % t) for t in range(PACK)]
         for t in range(PACK):
-            nc.scalar.copy(pos_win[t][:, N:], b_win[0][:, N:])
+            nc.scalar.activation(pos_win[t][:, N:], b_win[0][:, N:], ACT.Sigmoid)
 
         x2s = sb([P, N], U8, "x2s")
         gather(x2s[:], xs[:], l_two[:])
@@ -201,7 +200,6 @@ def tile_picked_ckqgatewindmix_none_po_kernel(tc, x_words, x_scales, d_words, d_
         ow = sb([P, N], I32, "ow")
         osc = sb([P, N], U8, "osc")
         neg5 = sb([P, PACK, N], F32, "neg5")
-        turned = sb([P, PACK, N], F32, "turned")
         res = sb([P, PACK, N], F32, "res")
         out_rows = out_0.rearrange("(p t) v -> p t v", t=PACK)
         out_words = out_1[0].rearrange("p c r -> p (c r)").bitcast(I32)
@@ -218,15 +216,16 @@ def tile_picked_ckqgatewindmix_none_po_kernel(tc, x_words, x_scales, d_words, d_
                 for i, term in enumerate(terms):
                     nc.tensor.matmul(sum_ps[:, P * k:P * (k + 1)], lhsT=term[:, P * k:P * (k + 1)], rhs=ident[:],
                                      is_transpose=True, start=(i == 0), stop=(i == len(terms) - 1))
-            nc.scalar.copy(turned[:, t, :], sum_ps[:])
+            turned = sb([P, N], F32, "turned%d" % t, "turned%d" % t)
+            nc.scalar.copy(turned[:], sum_ps[:])
             lead_ps = bank(t, "lead_ps%d" % t)
             for k in range(PACK):
-                nc.tensor.transpose(lead_ps[:, P * k:P * (k + 1)], turned[:, t, P * k:P * (k + 1)], ident[:])
+                nc.tensor.transpose(lead_ps[:, P * k:P * (k + 1)], turned[:, P * k:P * (k + 1)], ident[:])
             return lead_ps
 
         def gap_step(i):
             t, lo, hi = pieces[i]
-            gap = sb([P, hi - lo], F32, "gap%d" % i, "slot%d" % (2 + t % 2))
+            gap = sb([P, hi - lo], F32, "gap%d" % i, GAP_SLOTS[i])
             nc.vector.tensor_tensor(gap[:], neg_win[t][:].indirect(l_n6[:, lo // 16:hi // 16]),
                                     neg5[:, t, lo:hi], ALU.subtract)
             return gap

@@ -20,7 +20,7 @@ N = 512
 T = 1024
 G = 2048
 HALF = 256
-GAP_SLOTS = ("slot2", "slot3", "turned0", "turned1", "turned3")
+GAP_SLOTS = ("slot2", "slot3", "turned0", "turned1")
 FLOPS = 3 * 2 * 512 * 512 * 512
 
 
@@ -49,11 +49,6 @@ def tile_picked_ckqgatewindmix_none_po_kernel(tc, x_words, x_scales, d_words, d_
             for q in range(4):
                 view = rows[4 * q:4 * q + 4, :].unsqueeze(0).broadcast_to([8, 4, width // 4])
                 queue.dma_start(tile[:].bitcast(I32)[32 * q:32 * (q + 1), :], view)
-            return tile
-
-        def window(engine, name):
-            tile = sb([P, 2 * N], F32, name)
-            engine.memset(tile[:, N:], 0.0)
             return tile
 
         def load_words(src, words, name):
@@ -99,11 +94,13 @@ def tile_picked_ckqgatewindmix_none_po_kernel(tc, x_words, x_scales, d_words, d_
         make_identity(nc, ident[:])
         gcol = sb([P, 2 * PACK], F32, "gcol")
 
-        b_win = [window(nc.vector, "b_win%d" % t) for t in range(PACK)]
-        neg_win = [window(nc.gpsimd, "neg_win%d" % t) for t in range(PACK)]
-        pos_win = [sb([P, 2 * N], F32, "pos_win%d" % t) for t in range(PACK)]
-        for t in range(PACK):
-            nc.scalar.activation(pos_win[t][:, N:], b_win[0][:, N:], ACT.Sigmoid)
+        windows = [sb([P, 2 * N], F32, "window%d" % i) for i in range(3 * PACK)]
+        for i, win in enumerate(windows):
+            if i < PACK:
+                nc.vector.memset(win[:, N:], 0.0)
+            else:
+                nc.scalar.activation(win[:, N:], windows[0][:, N:], ACT.Sigmoid)
+        b_win, neg_win, pos_win = windows[:PACK], windows[PACK:2 * PACK], windows[2 * PACK:]
 
         x2s = sb([P, N], U8, "x2s")
         gather(x2s[:], xs[:], l_two[:])
@@ -194,8 +191,9 @@ def tile_picked_ckqgatewindmix_none_po_kernel(tc, x_words, x_scales, d_words, d_
                 s_ps[:],
                 lhsT=zw[h][:, P * u:P * (u + 1)].bitcast(FP8X4), lhsT_scale=zs[h][:, P * u:P * (u + 1)],
                 rhs=z2w[:].bitcast(FP8X4), rhs_scale=z2s[:], start=True, stop=True)
-            nc.scalar.activation(neg_win[t][:, :N], s_ps[:], ACT.Copy, scale=-0.0625)
-            nc.scalar.activation(pos_win[t][:, :N], s_ps[:], ACT.Copy, scale=0.0625)
+            copies = [(neg_win[t], -0.0625), (pos_win[t], 0.0625)]
+            for win, scale in copies if t == 0 else reversed(copies):
+                nc.scalar.activation(win[:, :N], s_ps[:], ACT.Copy, scale=scale)
 
         ow = sb([P, N], I32, "ow")
         osc = sb([P, N], U8, "osc")
@@ -205,9 +203,12 @@ def tile_picked_ckqgatewindmix_none_po_kernel(tc, x_words, x_scales, d_words, d_
         out_words = out_1[0].rearrange("p c r -> p (c r)").bitcast(I32)
 
         def lead(t):
-            gather(neg5[:, t, :], neg_win[t][:], l_n5[:])
+            if t == 0:
+                gather(neg5[:, t, :], neg_win[t][:], l_n5[:])
             rise = sb([P, N], F32, "rise%d" % t, "slot%d" % t)
             nc.vector.tensor_tensor(rise[:], pos_win[t][:].indirect(l_n4[:]), neg_win[t][:, :N], ALU.add)
+            if t > 0:
+                gather(neg5[:, t, :], neg_win[t][:], l_n5[:])
             excess = keep.tile([P, N], F32, name="excess%d" % t, tag="excess", bufs=2)
             nc.scalar.activation(excess[:], rise[:], ACT.Relu)
             sum_ps = bank(4 + t, "sum_ps%d" % t)
@@ -223,16 +224,13 @@ def tile_picked_ckqgatewindmix_none_po_kernel(tc, x_words, x_scales, d_words, d_
                 nc.tensor.transpose(lead_ps[:, P * k:P * (k + 1)], turned[:, P * k:P * (k + 1)], ident[:])
             return lead_ps
 
-        def gap_step(i):
-            t, lo, hi = pieces[i]
-            gap = sb([P, hi - lo], F32, "gap%d" % i, GAP_SLOTS[i])
-            nc.vector.tensor_tensor(gap[:], neg_win[t][:].indirect(l_n6[:, lo // 16:hi // 16]),
-                                    neg5[:, t, lo:hi], ALU.subtract)
+        def gap_step(t):
+            gap = sb([P, N], F32, "gap%d" % t, GAP_SLOTS[t])
+            nc.vector.tensor_tensor(gap[:], neg_win[t][:].indirect(l_n6[:]), neg5[:, t, :], ALU.subtract)
             return gap
 
-        def last_step(i, gap):
-            t, lo, hi = pieces[i]
-            nc.vector.scalar_tensor_tensor(res[:, t, lo:hi], gap[:], 0.0, leads[t][:, lo:hi], ALU.min, ALU.add)
+        def last_step(t, gap, lo, hi):
+            nc.vector.scalar_tensor_tensor(res[:, t, lo:hi], gap[:, lo:hi], 0.0, leads[t][:, lo:hi], ALU.min, ALU.add)
             nc.sync.dma_start(out_rows[:, t, lo:hi], res[:, t, lo:hi])
 
         def round_half(copy, h):
@@ -246,7 +244,6 @@ def tile_picked_ckqgatewindmix_none_po_kernel(tc, x_words, x_scales, d_words, d_
             nc.vector.quantize_mx(ow[:, cols].bitcast(FP8X4), osc[:, cols], rb[:])
             nc.sync.dma_start(out_words[:, cols], ow[:, cols])
 
-        pieces = [(0, 0, N), (1, 0, N), (2, 0, N), (3, 0, HALF), (3, HALF, N)]
         leads = []
         s_rows(0)
         for t in range(PACK):
@@ -254,16 +251,16 @@ def tile_picked_ckqgatewindmix_none_po_kernel(tc, x_words, x_scales, d_words, d_
                 s_rows(t + 1)
             leads.append(lead(t))
         gap = gap_step(0)
-        for i in range(PACK - 1):
-            next_gap = gap_step(i + 1)
-            last_step(i, gap)
+        for t in range(PACK - 1):
+            next_gap = gap_step(t + 1)
+            last_step(t, gap, 0, N)
             gap = next_gap
-        last_step(PACK - 1, gap)
+        last_step(PACK - 1, gap, 0, HALF)
         rb0 = round_half(nc.scalar.copy, 0)
-        last_step(PACK, gap_step(PACK))
+        last_step(PACK - 1, gap, HALF, N)
         rb1 = round_half(nc.vector.tensor_copy, 1)
-        planes(rb0, 0)
         planes(rb1, 1)
+        planes(rb0, 0)
         out_scales = out_2[0].bitcast(I32)
         for r in range(4):
             (nc.scalar, nc.sync)[r % 2].dma_start(out_scales[r:16:4, :], osc[:].bitcast(I32)[r:P:32, :])

from contextlib import ExitStack

import concourse.mybir as mybir
from concourse.masks import make_identity

F32 = mybir.dt.float32
BF16 = mybir.dt.bfloat16
I32 = mybir.dt.int32
U32 = mybir.dt.uint32
U16 = mybir.dt.uint16
U8 = mybir.dt.uint8
FP8X4 = mybir.dt.float8_e4m3fn_x4
FP4X4 = mybir.dt.float4_e2m1fn_x4
ALU = mybir.AluOpType
ACT = mybir.ActivationFunctionType

P = 128
PACK = 4
N = 512
T = 1024
G = 2048
HALF = 256
GAP_SLOTS = ("slot2", "slot3", "turned0", "turned1")
FLOPS = 3 * 2 * 512 * 512 * 512


def tile_picked_ckqgatewindmix_none_po_kernel(tc, x_words, x_scales, d_words, d_scales, w1_words, w1_scales, ga, gb,
        offs, k1, two, n1, n2, n3, n4, n5, n6, out_0, out_1, out_2):
    nc = tc.nc
    with ExitStack() as ctx:
        lists = ctx.enter_context(tc.tile_pool(name="lists", bufs=1))
        keep = ctx.enter_context(tc.tile_pool(name="keep", bufs=1))
        psum = ctx.enter_context(tc.psum_pool(name="psum", bufs=1))

        def sb(shape, dtype, name, tag=""):
            return keep.tile(shape, dtype, name=name, tag=tag or name, align_bytes=64)

        def bank(i, name):
            return psum.tile([P, N], F32, name=name, tag="bank%d" % i)

        def load_list(src, name):
            tile = lists.tile([P, N // 16], U16, name=name)
            nc.sync.dma_start(tile[:], src)
            return tile

        def load_plane(queue, src, width, name):
            tile = sb([P, width], U8, name)
            rows = src[0].bitcast(I32)
            for q in range(4):
                view = rows[4 * q:4 * q + 4, :].unsqueeze(0).broadcast_to([8, 4, width // 4])
                queue.dma_start(tile[:].bitcast(I32)[32 * q:32 * (q + 1), :], view)
            return tile

        def load_words(src, words, name):
            tile = sb([P, words], I32, name)
            nc.sync.dma_start(tile[:], src.bitcast(I32))
            return tile

        def gather(out, window, offsets):
            nc.vector.tensor_copy(out, window.indirect(offsets))

        def deal(src, run, name):
            width = src.shape[1]
            tile = sb([P, width], I32, name)
            nc.vector.tensor_copy(
                tile[:].rearrange("p (t b w) -> p t b w", t=PACK, w=run),
                src.rearrange("p (b t w) -> p t b w", t=PACK, w=run))
            return tile

        l_two = load_list(two, "l_two")
        xs = load_plane(nc.sync, x_scales, T, "xs")
        xw = load_words(x_words[0].rearrange("p c r -> p (c r)"), T, "xw")
        w1w = load_words(w1_words[0], N // 2, "w1w")
        l_k1 = load_list(k1, "l_k1")
        w1s = load_plane(nc.sync, w1_scales, N, "w1s")
        ds = sb([P, G], U8, "ds")
        nc.sync.dma_start(ds[:].bitcast(I32), d_scales[0].bitcast(I32).unsqueeze(1).broadcast_to([16, 8, G // 4]))
        l_offs = load_list(offs, "l_offs")
        dw = load_words(d_words[0].rearrange("p c r -> p (c r)"), G, "dw")
        l_n3 = load_list(n3, "l_n3")
        l_n2 = load_list(n2, "l_n2")
        l_n1 = load_list(n1, "l_n1")
        l_n4 = load_list(n4, "l_n4")
        l_n5 = load_list(n5, "l_n5")
        l_n6 = load_list(n6, "l_n6")

        grows = sb([P, P], F32, "grows")
        nc.gpsimd.memset(grows[:], 0.0)
        for i, g in enumerate((ga, gb)):
            nc.gpsimd.dma_start(
                grows[PACK * i:PACK * (i + 1), :].rearrange("t (b e) -> t b e", e=8),
                g.rearrange("(b t e) o -> t b (e o)", t=PACK, e=8))
        ident = sb([P, P], F32, "ident")
        make_identity(nc, ident[:])
        gcol = sb([P, 2 * PACK], F32, "gcol")

        windows = [sb([P, 2 * N], F32, "window%d" % i) for i in range(3 * PACK)]
        for i, win in enumerate(windows):
            if i < PACK:
                nc.vector.memset(win[:, N:], 0.0)
            else:
                nc.scalar.activation(win[:, N:], windows[0][:, N:], ACT.Sigmoid)
        b_win, neg_win, pos_win = windows[:PACK], windows[PACK:2 * PACK], windows[2 * PACK:]

        x2s = sb([P, N], U8, "x2s")
        gather(x2s[:], xs[:], l_two[:])
        x2w = sb([P, N], I32, "x2w")
        gather(x2w[:].bitcast(U32), xw[:].bitcast(U32), l_two[:])
        w1wd = deal(w1w[:], 4, "w1wd")
        w1sd = deal(w1s[:].bitcast(I32), 2, "w1sd")
        dsg = sb([P, N], U8, "dsg")
        gather(dsg[:], ds[:], l_k1[:])
        ds_odd = deal(dsg[:].bitcast(I32), 2, "ds_odd")
        dsd = deal(dsg[:].bitcast(I32), 2, "dsd")
        for r in range(1, 4):
            nc.sync.dma_start(dsd[r:P:32, :], ds_odd[8 * r:P:32, :])
        b_ps = [bank(t, "b_ps%d" % t) for t in range(PACK)]
        for t in range(PACK):
            nc.tensor.matmul_mx(
                b_ps[t][:],
                lhsT=w1wd[:].bitcast(U8)[:, 2 * P * t:2 * P * (t + 1)].bitcast(FP4X4),
                lhsT_scale=w1sd[:].bitcast(U8)[:, P * t:P * (t + 1)],
                rhs=x2w[:].bitcast(FP8X4), rhs_scale=x2s[:], start=True, stop=True)
            nc.scalar.activation(b_win[t][:, :N], b_ps[t][:], ACT.Copy)
        gps = bank(7, "gps")
        nc.tensor.transpose(gps[:, 0:P], grows[:], ident[:])
        nc.scalar.activation(gcol[:], gps[:, 0:2 * PACK], ACT.Copy)
        b_gain = sb([P, PACK, N], F32, "b_gain")
        for t in range(PACK):
            nc.scalar.activation(b_gain[:, t, :], b_ps[t][:], ACT.Copy, scale=gcol[:, PACK + t:PACK + t + 1])

        x1s = sb([P, N], U8, "x1s")
        gather(x1s[:], xs[:], l_offs[:])
        x1w = sb([P, N], I32, "x1w")
        gather(x1w[:].bitcast(U32), xw[:].bitcast(U32), l_offs[:])
        dwg = sb([P, N], I32, "dwg", "dwg_b3")
        gather(dwg[:].bitcast(U32), dw[:].bitcast(U32), l_k1[:])
        dwd = deal(dwg[:], 8, "dwd")
        a_win = [sb([P, N], F32, "a_win%d" % t) for t in range(PACK)]
        a_gain = sb([P, PACK, N], F32, "a_gain")
        gate = sb([P, PACK, N], F32, "gate")
        for t in range(PACK):
            a_ps = bank(4 + t, "a_ps%d" % t)
            nc.tensor.matmul_mx(
                a_ps[:],
                lhsT=dwd[:, P * t:P * (t + 1)].bitcast(FP8X4),
                lhsT_scale=dsd[:].bitcast(U8)[:, P * t:P * (t + 1)],
                rhs=x1w[:].bitcast(FP8X4), rhs_scale=x1s[:], start=True, stop=True)
            nc.scalar.activation(a_win[t][:], a_ps[:], ACT.Copy, scale=0.0625)
            for h in range(2):
                nc.scalar.activation(gate[:, t, HALF * h:HALF * (h + 1)],
                                     a_win[t][:].indirect(l_n1[:, 16 * h:16 * (h + 1)]), ACT.Sigmoid)
            nc.scalar.activation(a_gain[:, t, :], a_win[t][:], ACT.Copy, scale=gcol[:, t:t + 1])

        b3 = sb([P, PACK, N], F32, "b3", "dwg_b3")
        diff = sb([P, PACK, N], F32, "diff")
        for t in range(PACK):
            gather(b3[:, t, :], b_win[t][:], l_n3[:])
        for t in range(PACK):
            nc.vector.tensor_tensor(diff[:, t, :], b_win[t][:].indirect(l_n2[:]), b3[:, t, :], ALU.subtract)
        zb = [sb([P, HALF * PACK], BF16, "zb%d" % h) for h in range(2)]
        zw = [sb([P, HALF], I32, "zw%d" % h) for h in range(2)]
        zs = [sb([P, HALF], U8, "zs%d" % h) for h in range(2)]

        def z_product(h):
            nc.vector.tensor_tensor(
                zb[h][:].rearrange("p (u m t) -> p m t u", u=2, t=PACK),
                gate[:].rearrange("p t (m u) -> p m t u", u=PACK)[:, :, :, 2 * h:2 * h + 2],
                a_gain[:].rearrange("p t (m u) -> p m t u", u=PACK)[:, :, :, 2 * h:2 * h + 2], ALU.mult)

        def z_quantise(h):
            nc.vector.quantize_mx(zw[h][:].bitcast(FP8X4), zs[h][:], zb[h][:])

        z2b = sb([P, N * PACK], BF16, "z2b")
        z2w = sb([P, N], I32, "z2w")
        z2s = sb([P, N], U8, "z2s")
        nc.vector.tensor_tensor(
            z2b[:].rearrange("p (c i t) -> p c t i", i=2, t=PACK),
            diff[:].rearrange("p t (c i) -> p c t i", i=2),
            b_gain[:].rearrange("p t (c i) -> p c t i", i=2), ALU.mult)
        z_product(0)
        nc.vector.quantize_mx(z2w[:].bitcast(FP8X4), z2s[:], z2b[:])
        z_quantise(0)
        z_product(1)
        z_quantise(1)

        def s_rows(t):
            h, u = divmod(t, 2)
            s_ps = bank(t, "s_ps%d" % t)
            nc.tensor.matmul_mx(
                s_ps[:],
                lhsT=zw[h][:, P * u:P * (u + 1)].bitcast(FP8X4), lhsT_scale=zs[h][:, P * u:P * (u + 1)],
                rhs=z2w[:].bitcast(FP8X4), rhs_scale=z2s[:], start=True, stop=True)
            copies = [(neg_win[t], -0.0625), (pos_win[t], 0.0625)]
            for win, scale in copies if t == 0 else reversed(copies):
                nc.scalar.activation(win[:, :N], s_ps[:], ACT.Copy, scale=scale)

        ow = sb([P, N], I32, "ow")
        osc = sb([P, N], U8, "osc")
        neg5 = sb([P, PACK, N], F32, "neg5")
        res = sb([P, PACK, N], F32, "res")
        out_rows = out_0.rearrange("(p t) v -> p t v", t=PACK)
        out_words = out_1[0].rearrange("p c r -> p (c r)").bitcast(I32)

        def lead(t):
            if t == 0:
                gather(neg5[:, t, :], neg_win[t][:], l_n5[:])
            rise = sb([P, N], F32, "rise%d" % t, "slot%d" % t)
            nc.vector.tensor_tensor(rise[:], pos_win[t][:].indirect(l_n4[:]), neg_win[t][:, :N], ALU.add)
            if t > 0:
                gather(neg5[:, t, :], neg_win[t][:], l_n5[:])
            excess = keep.tile([P, N], F32, name="excess%d" % t, tag="excess", bufs=2)
            nc.scalar.activation(excess[:], rise[:], ACT.Relu)
            sum_ps = bank(4 + t, "sum_ps%d" % t)
            terms = (pos_win[t][:, :N], neg5[:, t, :], excess[:])
            for k in range(PACK):
                for i, term in enumerate(terms):
                    nc.tensor.matmul(sum_ps[:, P * k:P * (k + 1)], lhsT=term[:, P * k:P * (k + 1)], rhs=ident[:],
                                     is_transpose=True, start=(i == 0), stop=(i == len(terms) - 1))
            turned = sb([P, N], F32, "turned%d" % t, "turned%d" % t)
            nc.scalar.copy(turned[:], sum_ps[:])
            lead_ps = bank(t, "lead_ps%d" % t)
            for k in range(PACK):
                nc.tensor.transpose(lead_ps[:, P * k:P * (k + 1)], turned[:, P * k:P * (k + 1)], ident[:])
            return lead_ps

        def gap_step(t):
            gap = sb([P, N], F32, "gap%d" % t, GAP_SLOTS[t])
            nc.vector.tensor_tensor(gap[:], neg_win[t][:].indirect(l_n6[:]), neg5[:, t, :], ALU.subtract)
            return gap

        def last_step(t, gap, lo, hi):
            nc.vector.scalar_tensor_tensor(res[:, t, lo:hi], gap[:, lo:hi], 0.0, leads[t][:, lo:hi], ALU.min, ALU.add)
            nc.sync.dma_start(out_rows[:, t, lo:hi], res[:, t, lo:hi])

        def round_half(copy, h):
            rb = sb([P, HALF * PACK], BF16, "rb%d" % h)
            copy(rb[:].rearrange("p (c i t) -> p c t i", i=4, t=PACK),
                 res[:, :, HALF * h:HALF * (h + 1)].rearrange("p t (c i) -> p c t i", i=4))
            return rb

        def planes(rb, h):
            cols = slice(HALF * h, HALF * (h + 1))
            nc.vector.quantize_mx(ow[:, cols].bitcast(FP8X4), osc[:, cols], rb[:])
            nc.sync.dma_start(out_words[:, cols], ow[:, cols])

        leads = []
        s_rows(0)
        for t in range(PACK):
            if t + 1 < PACK:
                s_rows(t + 1)
            leads.append(lead(t))
        gap = gap_step(0)
        for t in range(PACK - 1):
            next_gap = gap_step(t + 1)
            last_step(t, gap, 0, N)
            gap = next_gap
        last_step(PACK - 1, gap, 0, HALF)
        rb0 = round_half(nc.scalar.copy, 0)
        last_step(PACK - 1, gap, HALF, N)
        rb1 = round_half(nc.vector.tensor_copy, 1)
        planes(rb1, 1)
        planes(rb0, 0)
        out_scales = out_2[0].bitcast(I32)
        for r in range(4):
            (nc.scalar, nc.sync)[r % 2].dma_start(out_scales[r:16:4, :], osc[:].bitcast(I32)[r:P:32, :])
